import numpy as np
import ml_dtypes


def mxq(x, axis, fmt="e4m3"):
    dtype, down = {"e4m3": (ml_dtypes.float8_e4m3fn, 7), "e5m2": (ml_dtypes.float8_e5m2, 14)}[fmt]
    v = np.moveaxis(np.asarray(x, np.float32).astype(ml_dtypes.bfloat16).astype(np.float64), axis, -1)
    blocks = v.reshape(v.shape[:-1] + (-1, 32))
    amax = np.abs(blocks).max(-1, keepdims=True)
    byte = np.maximum(np.where(amax > 0, np.frexp(amax)[1] - 1 + 127, 0) - down, 1)
    scale = np.exp2(byte - 127.0)
    codes = (blocks / scale).astype(np.float32).astype(dtype).astype(np.float64)
    return np.moveaxis((codes * scale).reshape(v.shape), -1, axis)


WIDE = False


def mx_kscale(k):
    if not WIDE:
        return np.ones(k)
    levels = np.array([10, -10, 5, -5, 0])
    if k % 512:
        return np.exp2(np.random.permutation(np.resize(levels, k // 32))).repeat(32)
    a = np.empty((k // 512, 16))
    for p in range(k // 512):
        a[p, :8] = np.random.permutation(np.resize(levels, 8))
        for g in range(8):
            far = levels[np.abs(levels - a[p, g]) >= 10]
            a[p, g + 8] = far[np.random.randint(len(far))]
    return np.exp2(a.ravel()).repeat(32)


BF16 = ml_dtypes.bfloat16


def bf(x):
    return np.asarray(x, np.float32).astype(BF16)


def f64(x):
    return np.asarray(x).astype(np.float64)


E2M1 = np.array([0.0, 0.5, 1.0, 1.5, 2.0, 3.0, 4.0, 6.0, -0.0, -0.5, -1.0, -1.5, -2.0, -3.0, -4.0, -6.0])


def pack_weight(w, fmt):
    k, n = w.shape
    w = f64(bf(w)).reshape(k // 32, 32, n)
    amax = np.abs(w).max(1)
    if fmt == "e4m3":
        byte = np.frexp(amax)[1] - 1 + 127 - 7
    else:
        mant, ex = np.frexp(amax / 6.0)
        byte = np.where(mant > 0.5, ex, ex - 1) + 127
    byte = np.clip(np.where(amax > 0, byte, 1), 1, 254)
    scaled = (w * np.exp2(127.0 - byte)[:, None, :]).reshape(k, n).astype(np.float32)
    by_word = np.ascontiguousarray(scaled.reshape(k // 512, 128, 4, n).transpose(0, 1, 3, 2))
    if fmt == "e4m3":
        words = by_word.astype(ml_dtypes.float8_e4m3fn).view(np.uint8)
    else:
        c = by_word.astype(ml_dtypes.float4_e2m1fn).view(np.uint8) & 0xF
        words = c[..., 0::2] | (c[..., 1::2] << 4)
    return np.ascontiguousarray(words), np.ascontiguousarray(byte.astype(np.uint8).reshape(k // 512, 16, n))


def unpack_weight(words, scales, fmt):
    g, p, n, _ = words.shape
    if fmt == "e4m3":
        vals = np.ascontiguousarray(words).view(ml_dtypes.float8_e4m3fn).astype(np.float64)
    else:
        nib = np.empty((g, p, n, 4), np.uint8)
        nib[..., 0::2] = words & 0xF
        nib[..., 1::2] = words >> 4
        vals = E2M1[nib]
    vals = vals * np.repeat(np.exp2(scales.astype(np.float64) - 127.0), 8, axis=1)[..., None]
    return vals.transpose(0, 1, 3, 2).reshape(g * 512, n)
def pack4(w):
    words, scales = pack_weight(w, "e2m1")
    return words.reshape(words.shape[0], 128, -1), scales


def unpack4(words, scales):
    return unpack_weight(words.reshape(words.shape[0], 128, -1, 2), scales, "e2m1")


E4M3FN = np.array([(-1.0 if i & 128 else 1.0) * ((1.0 + (i & 7) / 8.0) * 2.0 ** (((i >> 3) & 15) - 7) if i & 120 else (i & 7) * 2.0 ** -9) for i in range(256)])


def e4m3fn_bytes(y):
    return np.clip(np.asarray(y, np.float64), -448.0, 448.0).astype(np.float32).astype(ml_dtypes.float8_e4m3fn).view(np.uint8)


def e4m3fn_values(b):
    return E4M3FN[b]


T, K, V, N, B = 1024, 1024, 2048, 1024, 128


def setup_inputs():
    s, t = mx_kscale(K), mx_kscale(V)
    x = np.random.standard_normal((T, K)) * s
    x_scale = (np.abs(x).reshape(T, K // B, B).max(axis=2) / 448.0).astype(np.float32)
    x_bytes = e4m3fn_bytes(x / np.repeat(f64(x_scale), B, axis=1))
    head = np.random.standard_normal((V, K)) / np.sqrt(K) / s * t[:, None]
    vmap = np.random.standard_normal((V, N)) / np.sqrt(V) / t[:, None]
    map_words, map_scales = pack4(vmap)
    return {"x_bytes": x_bytes,
            "x_scale": x_scale,
            "head": bf(head),
            "b": bf(0.4 * np.random.standard_normal(V) * t),
            "tau": bf(np.random.uniform(1.0, 3.0, T)),
            "map_words": map_words,
            "map_scales": map_scales,
            "c": bf(0.3 * np.random.standard_normal(N))}


def reference(x_bytes, x_scale, head, b, tau, map_words, map_scales, c):
    x = e4m3fn_values(x_bytes) * np.repeat(f64(x_scale), B, axis=1)
    logits = mxq(x, 1, "e4m3") @ mxq(f64(head), 1, "e4m3").T
    z = (logits + f64(b)) / f64(tau)[:, None]
    y = mxq(z, 1, "e4m3") @ unpack4(map_words, map_scales)
    return y + f64(c)

from contextlib import ExitStack

import concourse.mybir as mybir
from concourse.masks import make_identity

T, K, V, N, B = 1024, 1024, 2048, 1024, 128
FLOPS = 2 * T * K * V + 2 * T * V * N

F32 = mybir.dt.float32
BF16 = mybir.dt.bfloat16
I32 = mybir.dt.int32
U32 = mybir.dt.uint32
U8 = mybir.dt.uint8
FP8 = mybir.dt.float8_e4m3fn
FP8X4 = mybir.dt.float8_e4m3fn_x4
FP4X4 = mybir.dt.float4_e2m1fn_x4
COPY = mybir.ActivationFunctionType.Copy
IDENT = mybir.ActivationFunctionType.Identity
ADD = mybir.AluOpType.add
MULT = mybir.AluOpType.mult

P = 128
G = 2
TT = 8
C = 4
S = 4
GROUPS = (4, 4)
WID = ["s","v","s","sv","s","sv","v","s"]
XCP = "svsvssss"
HCP = "vsvsvssvsvsvssss"
ZI = "ssssssss"
ORDER = [("r", 0), ("h", 0), ("h", 1), ("h", 2), ("x", 0), ("h", 3), ("x", 1), ("z", (0, 0)), ("z", (1, 0)), ("z", (2, 0)), ("z", (3, 0)), ("y", 0), ("z", (1, 1)), ("z", (2, 1)), ("y", 1), ("z", (0, 1)), ("z", (3, 1)), ("y", 2), ("y", 3), ("y", 4), ("y", 5), ("y", 6), ("y", 7)]
TPB = 3
A1B = 3
LOADS = [("x", 0), ("t", 0), ("x", 1), ("h", 0), ("h", 1), ("b", 0), ("h", 2), ("h", 3), ("h", 4), ("h", 5), ("x", 2), ("x", 3), ("h", 6), ("h", 7)]


def tile_teacher_logits_remap_d4_kernel(tc, x_bytes, x_scale, head, b, tau, map_words, map_scales, c, out):
    nc = tc.nc
    x_v = x_bytes.rearrange("(p i) k -> p i k", i=TT)
    head_v = head.rearrange("(c p s) k -> c p s k", p=P, s=S)
    out_v = out.rearrange("(p i) n -> p i n", i=TT)

    with ExitStack() as ctx:
        keep = ctx.enter_context(tc.tile_pool(name="keep", bufs=1))
        work = ctx.enter_context(tc.tile_pool(name="work", bufs=3))
        psum = ctx.enter_context(tc.psum_pool(name="psum", bufs=1))

        xs = keep.tile([P, TT, K // B], F32, name="xs")
        nc.sync.dma_start(out=xs[:], in_=x_scale.rearrange("(p i) j -> p i j", i=TT))
        xb = []
        for q in range(4):
            xb_q = keep.tile([P, 2, K], U8, name=f"xb{q}")
            xb.append(xb_q)
        hraw = []
        for e in range(2 * C):
            h_t = keep.tile([P, 2, K], BF16, name=f"hraw{e}")
            hraw.append(h_t)
        b_bf = keep.tile([P, C, S], BF16, name="b_bf")
        tau_sb = keep.tile([P, TT], BF16, name="tau_sb")
        msc = keep.tile([P, C, N], U8, name="msc", align_bytes=64)
        mw = keep.tile([P, C, 2 * N], U8, name="mw", align_bytes=64)
        c_bc = keep.tile([P, N], BF16, name="c_bc")

        def load_x(q):
            nc.sync.dma_start(out=xb[q][:], in_=x_v[:, 2 * q : 2 * q + 2, :])

        for what, arg in LOADS:
            if what == "x":
                load_x(arg)
            if what == "t":
                nc.sync.dma_start(out=tau_sb[:], in_=tau.rearrange("(p i) -> p i", i=TT))
            if what == "b":
                nc.sync.dma_start(out=b_bf[:], in_=b.rearrange("(c p s) -> p c s", p=P, s=S))
            if what == "h":
                nc.sync.dma_start(out=hraw[arg][:], in_=head_v[arg // 2, :, 2 * (arg % 2) : 2 * (arg % 2) + 2, :])
        nc.vector.memset(msc[:].rearrange("p c n -> p (c n)").bitcast(I32), 0)
        for q in range(4):
            nc.sync.dma_start(
                out=msc[32 * q : 32 * q + 4, :, :].bitcast(I32),
                in_=map_scales[:, 4 * q : 4 * q + 4, :].rearrange("c r n -> r c n").bitcast(I32),
            )
        nc.sync.dma_start(out=mw[:].bitcast(I32), in_=map_words.rearrange("c p n -> p c n").bitcast(I32))
        nc.sync.dma_start(out=c_bc[:], in_=c.partition_broadcast(P))

        ident = keep.tile([P, P], F32, name="ident")
        make_identity(nc, ident[:])

        rt_col = keep.tile([P, TT], F32, name="rt_col")
        b_sb = keep.tile([P, C, S], F32, name="b_sb")
        rtau = keep.tile([P, TT, P], F32, name="rtau")

        def make_rtau():
            nc.vector.reciprocal(rt_col[:], tau_sb[:])
            for i0 in range(0, TT, 4):
                rp = psum.tile([P, 4, P], F32, name="tp", tag="tp", bufs=3)
                for ii in range(4):
                    nc.tensor.transpose(rp[:, ii, :], rt_col[:, i0 + ii : i0 + ii + 1].to_broadcast([P, P]), ident[:])
                nc.scalar.copy(rtau[:, i0 : i0 + 4, :], rp[:])

        first = [sum(GROUPS[:h]) for h in range(len(GROUPS))]
        group_of = [h for h in range(len(GROUPS)) for ii in range(GROUPS[h])]
        xT = []
        xc = []
        xsc = []
        for h in range(len(GROUPS)):
            n = GROUPS[h] * P
            xt_h = keep.tile([P, G, n, 4], BF16, name=f"xT{h}", align_bytes=64)
            xc_h = keep.tile([P, G, n], U32, name=f"xc{h}", align_bytes=64)
            xsc_h = keep.tile([P, G, n], U8, name=f"xsc{h}", align_bytes=64)
            xT.append(xt_h)
            xc.append(xc_h)
            xsc.append(xsc_h)

        xw = [None] * TT

        def widen(i, eng):
            xw_i = work.tile([P, K], BF16, name="xw", bufs=4)
            xw[i] = xw_i
            for j in range(K // B):
                src = xb[i // 2][:, i % 2, j * B : (j + 1) * B].bitcast(FP8)
                if (j % 2 == 0) if eng == "sv" else (eng == "s"):
                    nc.scalar.activation(xw_i[:, j * B : (j + 1) * B], src, COPY, scale=xs[:, i, j : j + 1])
                else:
                    nc.vector.tensor_scalar(xw_i[:, j * B : (j + 1) * B], src, xs[:, i, j : j + 1], None, op0=MULT)

        def turn(words, copy_eng, dst):
            tp = psum.tile([P, G, 2, P], F32, name="tp", tag="tp", bufs=3)
            for g in range(G):
                for u in range(2):
                    nc.tensor.transpose(tp[:, g, u, :], words[:, 256 * g + u : 256 * (g + 1) : 2], ident[:])
            copy_eng(dst, tp[:].rearrange("p g u r -> p g r u"))

        def x_turn(i, copy_eng):
            h = group_of[i]
            ii = i - first[h]
            dst = xT[h][:, :, ii * P : (ii + 1) * P, :].rearrange("p g r t -> p g (r t)").bitcast(F32)
            turn(xw[i][:].bitcast(F32), copy_eng, dst.rearrange("p g (r u) -> p g r u", u=2))

        def x_quant(h):
            for g in range(G):
                nc.vector.quantize_mx(
                    out=xc[h][:, g, :].bitcast(FP8X4), scales=xsc[h][:, g, :], in_=xT[h][:, g, :, :].rearrange("p n t -> p (n t)")
                )

        hT = [None] * (2 * C)
        hc = []
        hs = []
        for e in range(2 * C):
            hc_e = keep.tile([P, 2, G, P], U32, name=f"hc{e}", align_bytes=64)
            hs_e = keep.tile([P, 2, G, P], U8, name=f"hs{e}", align_bytes=64)
            hc.append(hc_e)
            hs.append(hs_e)

        def head_turn(cc, s, copy_eng):
            e = 2 * cc + s // 2
            if s % 2 == 0:
                hT_e = work.tile([P, 2, G, P, 4], BF16, name="hT", align_bytes=64, bufs=4)
                hT[e] = hT_e
            dst = hT[e][:, s % 2].rearrange("p g r t -> p (g r t)").bitcast(F32)
            turn(hraw[e][:, s % 2, :].bitcast(F32), copy_eng, dst.rearrange("p (g r u) -> p g r u", g=G, u=2))

        def head_quant(cc, sp):
            e = 2 * cc + sp
            nc.vector.quantize_mx(
                out=hc[e][:].rearrange("p s g m -> p (s g m)").bitcast(FP8X4),
                scales=hs[e][:].rearrange("p s g m -> p (s g m)"),
                in_=hT[e][:].rearrange("p s g m t -> p (s g m t)"),
            )

        zp = {}
        zi = {}
        zc = {}
        zs = {}

        def stage1(cc, h, s):
            n = GROUPS[h] * P
            if s == 0:
                zp_t = work.tile([P, S, n], BF16, name="zp", bufs=3)
                zp[cc, h] = zp_t
            acc = psum.tile([P, n], F32, name="acc1", tag="acc1", bufs=3)
            e = 2 * cc + s // 2
            for g in range(G):
                nc.tensor.matmul_mx(
                    out=acc[:],
                    lhsT=hc[e][:, s % 2, g, :].bitcast(FP8X4),
                    lhsT_scale=hs[e][:, s % 2, g, :],
                    rhs=xc[h][:, g, :].bitcast(FP8X4),
                    rhs_scale=xsc[h][:, g, :],
                    start=(g == 0),
                    stop=(g == G - 1),
                )
            nc.vector.scalar_tensor_tensor(
                zp[cc, h][:, s, :],
                acc[:],
                b_sb[:, cc, s : s + 1],
                rtau[:, first[h] : first[h] + GROUPS[h], :].rearrange("p i n -> p (i n)"),
                op0=ADD,
                op1=MULT,
            )

        def z_inter(cc, h, copy_eng):
            n = GROUPS[h] * P
            zi_t = work.tile([P, n, S], BF16, name="zi", align_bytes=64, bufs=3)
            zi[cc, h] = zi_t
            copy_eng(
                zi_t[:].rearrange("p (n i) s -> p n s i", i=4),
                zp[cc, h][:].rearrange("p s (n i) -> p n s i", i=4),
            )

        def z_quant(cc, h):
            n = GROUPS[h] * P
            zc_t = keep.tile([P, n], U32, name=f"zc{cc}_{h}", align_bytes=64)
            zs_t = keep.tile([P, n], U8, name=f"zs{cc}_{h}", align_bytes=64)
            zc[cc, h] = zc_t
            zs[cc, h] = zs_t
            nc.vector.quantize_mx(out=zc_t[:].bitcast(FP8X4), scales=zs_t[:], in_=zi[cc, h][:].rearrange("p n s -> p (n s)"))

        yt = {}

        def stage2(i, nh):
            h = group_of[i]
            ii = i - first[h]
            cols = slice(ii * P, (ii + 1) * P)
            if nh == 0:
                y = work.tile([P, N], F32, name="y", bufs=3)
                yt[i] = y
            acc = psum.tile([P, 512], F32, name="acc2", tag="acc2", bufs=2)
            n0 = 512 * nh
            for cc in range(C):
                nc.tensor.matmul_mx(
                    out=acc[:],
                    lhsT=zc[cc, h][:, cols].bitcast(FP8X4),
                    lhsT_scale=zs[cc, h][:, cols],
                    rhs=mw[:, cc, 2 * n0 : 2 * n0 + 1024].bitcast(FP4X4),
                    rhs_scale=msc[:, cc, n0 : n0 + 512],
                    start=(cc == 0),
                    stop=(cc == C - 1),
                )
            nc.vector.tensor_tensor(yt[i][:, n0 : n0 + 512], acc[:], c_bc[:, n0 : n0 + 512], op=ADD)
            nc.sync.dma_start(out=out_v[:, i, n0 : n0 + 512], in_=yt[i][:, n0 : n0 + 512])

        sc, ve = nc.scalar.copy, nc.vector.tensor_copy
        eng = {"s": nc.scalar.copy, "v": nc.vector.tensor_copy}

        def head_prep(cc):
            for s in range(S):
                head_turn(cc, s, eng[HCP[4 * cc + s]])
                if s % 2 == 1:
                    head_quant(cc, s // 2)

        def x_prep(h):
            for i in range(first[h], first[h] + GROUPS[h]):
                widen(i, WID[i])
            for i in range(first[h], first[h] + GROUPS[h]):
                x_turn(i, eng[XCP[i]])
            x_quant(h)

        def z_unit(cc, h):
            for s in range(S):
                stage1(cc, h, s)
            z_inter(cc, h, eng[ZI[4 * h + cc]])
            z_quant(cc, h)

        for what, arg in ORDER:
            if what == "x":
                x_prep(arg)
            if what == "r":
                make_rtau()
                nc.vector.tensor_copy(b_sb[:], b_bf[:])
            if what == "h":
                head_prep(arg)
            if what == "z":
                z_unit(*arg)
            if what == "y":
                stage2(arg, 0)
                stage2(arg, 1)
